import numpy as np, ml_dtypes
CORES = [44,45,46,47,172,173,174,175,300,301,302,303,428,429,430,431]
N = 16
C = 64
def setup_inputs(rng):
    u = np.triu(np.ones((128, 128), np.float32)).astype(ml_dtypes.bfloat16)
    return {"x": rng.standard_normal((N, 128, C), dtype=np.float32).astype(ml_dtypes.bfloat16), "u": np.broadcast_to(u, (N, 128, 128)).copy()}
def setup_inputs_big(rng):
    d = setup_inputs(rng)
    for k in ("x", "u"): d[k] = (d[k].astype(np.float32) * 1024.0).astype(d[k].dtype)
    return d
def setup_inputs_small(rng):
    d = setup_inputs(rng)
    for k in ("x", "u"): d[k] = (d[k].astype(np.float32) * (1 / 1024.0)).astype(d[k].dtype)
    return d
def setup_inputs_apart(rng):
    d = setup_inputs(rng)
    f = (10.0 ** rng.permutation(np.linspace(-1.5, 1.5, N))).astype(np.float32).reshape(N, 1, 1)
    for k in ("x",): d[k] = (d[k].astype(np.float32) * f).astype(d[k].dtype)
    return d
def reference(x, u):
    X, U = x.astype(np.float64), u.astype(np.float64)
    y = np.zeros((N, 128, C)); c = np.zeros(C)
    for r in range(N):
        y[r] = U[r].T @ X[r] + c
        c = c + X[r].sum(axis=0)
    return {"y": y.astype(ml_dtypes.bfloat16)}

@@ -1,0 +1,125 @@
+from concourse.bass import DstId, RemoteDMATransfer
+
+C = 64
+W = 4
+PIECES = C // W
+ROWS = 2 * W
+SLOTS = 12
+HOSTS = 4
+
+SCRATCH = {
+    "xd": ("dram", [PIECES, 128, W], "bfloat16"),
+    "land": ("dram", [SLOTS, 128, W], "bfloat16"),
+    "xs": ("sbuf", [128, C], "bfloat16"),
+    "us": ("sbuf", [128, 128], "bfloat16"),
+    "ones": ("sbuf", [128, 128], "bfloat16"),
+    "lb": ("sbuf", [128, C], "bfloat16"),
+    "ys": ("sbuf", [128, C], "bfloat16"),
+    "yp": ("psum", [128, 512], "float32"),
+}
+SEMAPHORES = ["copied", "loaded", "filled", "gathered", "summed", "rounded", "stored", "sent", "arrf"] + [
+    "arr%d" % h for h in range(HOSTS)]
+
+
+def _inboxes(cores, topo):
+    n = len(cores)
+
+    def ok(a, b):
+        return topo.may_write(cores[a], cores[b])
+
+    inbox = []
+    for r in range(n):
+        near = [q for q in range(r) if ok(q, r)]
+        far = [q for q in range(r) if not ok(q, r)]
+        box = [(q, (q,)) for q in near]
+        if far:
+            relays = [m for m in near if all(q < m and ok(q, m) for q in far)]
+            peers = [p for p in range(n) if topo.host(cores[p]) == topo.host(cores[r])]
+            box.append((relays[peers.index(r) % len(relays)], tuple(far)))
+        inbox.append(box)
+    return inbox
+
+
+def _engine(topo, core, dests):
+    m = topo.mask(core, dests[0])
+    for d in dests:
+        m &= topo.mask(core, d)
+    return m & -m
+
+
+def rank_program(g, core, T, topo):
+    rank = T.rank_of(core)
+    if rank is None:
+        return
+    cores = list(T.cores)
+    n = len(cores)
+    sem = T.sem
+    inbox = _inboxes(cores, topo)
+    box = inbox[rank]
+    k = ROWS * len(box)
+
+    def same_chip(a, b):
+        return topo.host(a) == topo.host(b) and topo.chip(a) == topo.chip(b)
+
+    own = [(r, s) for r in range(n) for s, (m, qs) in enumerate(inbox[r]) if m == rank and qs == (rank,)]
+    passed = [(r, s, qs) for r in range(n) for s, (m, qs) in enumerate(inbox[r]) if m == rank and qs != (rank,)]
+    relays_me = set(m for b in inbox for (m, qs) in b if rank in qs and m != rank)
+    own.sort(key=lambda e: (e[0] not in relays_me, same_chip(core, cores[e[0]]), e[0]))
+    due = {}
+    for m, qs in box:
+        name = "arr%d" % topo.host(cores[m]) if qs == (m,) else "arrf"
+        due[name] = due.get(name, 0) + 1
+
+    if own:
+        g.sync.dma_start(T.xd[:], T.x[:]).then_inc(sem.copied, 16)
+    g.scalar.dma_start(T.xs[:], T.x[:]).then_inc(sem.loaded, 16)
+    g.scalar.dma_start(T.us[:], T.u[:]).then_inc(sem.loaded, 16)
+    if box:
+        g.vector.memset(T.ones[0:k, :], 1.0).then_inc(sem.filled, 1)
+
+    def ids(dests):
+        out = []
+        for d in dests:
+            rid, pid = topo.addr(d, core)
+            out.append(DstId(rid=rid, pnc=pid))
+        return out
+
+    sent = 0
+    if own:
+        dests = [cores[r] for r, s in own]
+        g.wait_ge(sem.copied, 16)
+        g.remote_dma_fused([RemoteDMATransfer(
+            dst_ids=ids(dests), dma_engine_mask=_engine(topo, core, dests),
+            remote_sem=sem["arr%d" % topo.host(core)],
+            srcs=[T.xd[t] for t in range(PIECES)], dsts=[T.land[s] for r, s in own], alu_op=1)], local_sem=sem.sent)
+        sent += 1
+    for r, s, qs in passed:
+        slots = [i for i, (m, ms) in enumerate(box) if ms == (m,) and m in qs]
+        for name in sorted(set("arr%d" % topo.host(cores[q]) for q in qs)):
+            g.wait_ge(sem[name], due[name])
+        g.remote_dma_fused([RemoteDMATransfer(
+            dst_ids=ids([cores[r]]), dma_engine_mask=_engine(topo, core, [cores[r]]), remote_sem=sem.arrf,
+            srcs=[T.land[i] for i in slots], dsts=[T.land[s]], alu_op=1 if len(slots) > 1 else 0)],
+            local_sem=sem.sent)
+        sent += 1
+    if sent:
+        g.wait_ge(sem.sent, sent)
+
+    if box:
+        for name in sorted(due):
+            g.sync.wait_ge(sem[name], due[name])
+        g.sync.dma_start(T.lb[0:k, :], T.land[0:len(box)]).then_inc(sem.gathered, 16)
+
+    g.tensor.wait_ge(sem.loaded, 32)
+    mm = g.tensor.matmul(T.yp[:, 0:C], T.us[:], T.xs[:], True, not box)
+    if box:
+        g.tensor.wait_ge(sem.filled, 1)
+        g.tensor.wait_ge(sem.gathered, 16)
+        mm = g.tensor.matmul(T.yp[:, 0:C], T.ones[0:k, :], T.lb[0:k, :], False, True)
+    mm.then_inc(sem.summed, 1)
+
+    g.vector.wait_ge(sem.summed, 1)
+    g.vector.tensor_copy(T.ys[:], T.yp[:, 0:C]).then_inc(sem.rounded, 1)
+    g.scalar.wait_ge(sem.rounded, 1)
+    g.scalar.dma_start(T.y[:], T.ys[:]).then_inc(sem.stored, 16)
+    g.scalar.wait_ge(sem.stored, 16)

@@ -4,20 +4,23 @@ C = 64
 W = 4
 PIECES = C // W
 ROWS = 2 * W
-SLOTS = 12
+SLOTS = 11
 HOSTS = 4
+E = 8
 
 SCRATCH = {
     "xd": ("dram", [PIECES, 128, W], "bfloat16"),
     "land": ("dram", [SLOTS, 128, W], "bfloat16"),
+    "farl": ("dram", [128, W], "bfloat16"),
     "xs": ("sbuf", [128, C], "bfloat16"),
     "us": ("sbuf", [128, 128], "bfloat16"),
     "ones": ("sbuf", [128, 128], "bfloat16"),
     "lb": ("sbuf", [128, C], "bfloat16"),
+    "fb": ("sbuf", [128, C], "bfloat16"),
     "ys": ("sbuf", [128, C], "bfloat16"),
     "yp": ("psum", [128, 512], "float32"),
 }
-SEMAPHORES = ["copied", "loaded", "filled", "gathered", "summed", "rounded", "stored", "sent", "arrf"] + [
+SEMAPHORES = ["copied", "loaded", "filled", "gathered", "fetched", "summed", "rounded", "stored", "sent", "arrf"] + [
     "arr%d" % h for h in range(HOSTS)]
 
 
@@ -27,24 +30,25 @@ def _inboxes(cores, topo):
     def ok(a, b):
         return topo.may_write(cores[a], cores[b])
 
-    inbox = []
+    near, far, via = [], [], []
     for r in range(n):
-        near = [q for q in range(r) if ok(q, r)]
-        far = [q for q in range(r) if not ok(q, r)]
-        box = [(q, (q,)) for q in near]
-        if far:
-            relays = [m for m in near if all(q < m and ok(q, m) for q in far)]
-            peers = [p for p in range(n) if topo.host(cores[p]) == topo.host(cores[r])]
-            box.append((relays[peers.index(r) % len(relays)], tuple(far)))
-        inbox.append(box)
-    return inbox
+        near.append([q for q in range(r) if ok(q, r)])
+        far.append([q for q in range(r) if not ok(q, r)])
+        relays = [m for m in near[r] if topo.host(cores[m]) != topo.host(cores[r])
+                  and all(q < m and ok(q, m) for q in far[r])]
+        via.append(relays[-1] if far[r] else None)
+    return near, far, via
 
 
-def _engine(topo, core, dests):
+def _engines(topo, core, dests):
     m = topo.mask(core, dests[0])
     for d in dests:
         m &= topo.mask(core, d)
-    return m & -m
+    out = 0
+    for _ in range(E):
+        out |= m & -m
+        m &= m - 1
+    return out
 
 
 def rank_program(g, core, T, topo):
@@ -54,24 +58,28 @@ def rank_program(g, core, T, topo):
     cores = list(T.cores)
     n = len(cores)
     sem = T.sem
-    inbox = _inboxes(cores, topo)
-    box = inbox[rank]
+    near, far, via = _inboxes(cores, topo)
+    box = near[rank]
     k = ROWS * len(box)
+    late = via[rank] is not None
 
     def same_chip(a, b):
         return topo.host(a) == topo.host(b) and topo.chip(a) == topo.chip(b)
 
-    own = [(r, s) for r in range(n) for s, (m, qs) in enumerate(inbox[r]) if m == rank and qs == (rank,)]
-    passed = [(r, s, qs) for r in range(n) for s, (m, qs) in enumerate(inbox[r]) if m == rank and qs != (rank,)]
-    relays_me = set(m for b in inbox for (m, qs) in b if rank in qs and m != rank)
-    own.sort(key=lambda e: (e[0] not in relays_me, same_chip(core, cores[e[0]]), e[0]))
+    def arr(q):
+        return "arr%d" % topo.host(cores[q])
+
+    own = [(r, near[r].index(rank)) for r in range(n) if rank in near[r]]
+    passes_me = set(via[r] for r in range(n) if rank in far[r])
+    own.sort(key=lambda e: (e[0] not in passes_me, same_chip(core, cores[e[0]]), e[0]))
+    served = [r for r in range(n) if via[r] == rank]
     due = {}
-    for m, qs in box:
-        name = "arr%d" % topo.host(cores[m]) if qs == (m,) else "arrf"
-        due[name] = due.get(name, 0) + 1
+    for q in box:
+        due[arr(q)] = due.get(arr(q), 0) + E
 
     if own:
         g.sync.dma_start(T.xd[:], T.x[:]).then_inc(sem.copied, 16)
+        g.scalar.wait_ge(sem.copied, 16)
     g.scalar.dma_start(T.xs[:], T.x[:]).then_inc(sem.loaded, 16)
     g.scalar.dma_start(T.us[:], T.u[:]).then_inc(sem.loaded, 16)
     if box:
@@ -89,19 +97,19 @@ def rank_program(g, core, T, topo):
         dests = [cores[r] for r, s in own]
         g.wait_ge(sem.copied, 16)
         g.remote_dma_fused([RemoteDMATransfer(
-            dst_ids=ids(dests), dma_engine_mask=_engine(topo, core, dests),
-            remote_sem=sem["arr%d" % topo.host(core)],
+            dst_ids=ids(dests), dma_engine_mask=_engines(topo, core, dests), remote_sem=sem[arr(rank)],
             srcs=[T.xd[t] for t in range(PIECES)], dsts=[T.land[s] for r, s in own], alu_op=1)], local_sem=sem.sent)
-        sent += 1
-    for r, s, qs in passed:
-        slots = [i for i, (m, ms) in enumerate(box) if ms == (m,) and m in qs]
-        for name in sorted(set("arr%d" % topo.host(cores[q]) for q in qs)):
+        sent += E
+    if served:
+        qs = far[served[0]]
+        dests = [cores[r] for r in served]
+        for name in sorted(set(arr(q) for q in qs)):
             g.wait_ge(sem[name], due[name])
         g.remote_dma_fused([RemoteDMATransfer(
-            dst_ids=ids([cores[r]]), dma_engine_mask=_engine(topo, core, [cores[r]]), remote_sem=sem.arrf,
-            srcs=[T.land[i] for i in slots], dsts=[T.land[s]], alu_op=1 if len(slots) > 1 else 0)],
-            local_sem=sem.sent)
-        sent += 1
+            dst_ids=ids(dests), dma_engine_mask=_engines(topo, core, dests), remote_sem=sem.arrf,
+            srcs=[T.land[box.index(q)] for q in qs], dsts=[T.farl[:] for r in served],
+            alu_op=1 if len(qs) > 1 else 0)], local_sem=sem.sent)
+        sent += E
     if sent:
         g.wait_ge(sem.sent, sent)
 
@@ -109,13 +117,19 @@ def rank_program(g, core, T, topo):
         for name in sorted(due):
             g.sync.wait_ge(sem[name], due[name])
         g.sync.dma_start(T.lb[0:k, :], T.land[0:len(box)]).then_inc(sem.gathered, 16)
+    if late:
+        g.scalar.wait_ge(sem.arrf, E)
+        g.scalar.dma_start(T.fb[0:ROWS, :], T.farl[:]).then_inc(sem.fetched, 16)
 
     g.tensor.wait_ge(sem.loaded, 32)
     mm = g.tensor.matmul(T.yp[:, 0:C], T.us[:], T.xs[:], True, not box)
     if box:
         g.tensor.wait_ge(sem.filled, 1)
         g.tensor.wait_ge(sem.gathered, 16)
-        mm = g.tensor.matmul(T.yp[:, 0:C], T.ones[0:k, :], T.lb[0:k, :], False, True)
+        mm = g.tensor.matmul(T.yp[:, 0:C], T.ones[0:k, :], T.lb[0:k, :], False, not late)
+    if late:
+        g.tensor.wait_ge(sem.fetched, 16)
+        mm = g.tensor.matmul(T.yp[:, 0:C], T.ones[0:ROWS, :], T.fb[0:ROWS, :], False, True)
     mm.then_inc(sem.summed, 1)
 
     g.vector.wait_ge(sem.summed, 1)

from concourse.bass import DstId, RemoteDMATransfer

C = 64
W = 4
PIECES = C // W
ROWS = 2 * W
SLOTS = 11
HOSTS = 4
E = 8

SCRATCH = {
    "xd": ("dram", [PIECES, 128, W], "bfloat16"),
    "land": ("dram", [SLOTS, 128, W], "bfloat16"),
    "farl": ("dram", [128, W], "bfloat16"),
    "xs": ("sbuf", [128, C], "bfloat16"),
    "us": ("sbuf", [128, 128], "bfloat16"),
    "ones": ("sbuf", [128, 128], "bfloat16"),
    "lb": ("sbuf", [128, C], "bfloat16"),
    "fb": ("sbuf", [128, C], "bfloat16"),
    "ys": ("sbuf", [128, C], "bfloat16"),
    "yp": ("psum", [128, 512], "float32"),
}
SEMAPHORES = ["copied", "loaded", "filled", "gathered", "fetched", "summed", "rounded", "stored", "sent", "arrf"] + [
    "arr%d" % h for h in range(HOSTS)]


def _inboxes(cores, topo):
    n = len(cores)

    def ok(a, b):
        return topo.may_write(cores[a], cores[b])

    near, far, via = [], [], []
    for r in range(n):
        near.append([q for q in range(r) if ok(q, r)])
        far.append([q for q in range(r) if not ok(q, r)])
        relays = [m for m in near[r] if topo.host(cores[m]) != topo.host(cores[r])
                  and all(q < m and ok(q, m) for q in far[r])]
        via.append(relays[-1] if far[r] else None)
    return near, far, via


def _engines(topo, core, dests):
    m = topo.mask(core, dests[0])
    for d in dests:
        m &= topo.mask(core, d)
    out = 0
    for _ in range(E):
        out |= m & -m
        m &= m - 1
    return out


def rank_program(g, core, T, topo):
    rank = T.rank_of(core)
    if rank is None:
        return
    cores = list(T.cores)
    n = len(cores)
    sem = T.sem
    near, far, via = _inboxes(cores, topo)
    box = near[rank]
    k = ROWS * len(box)
    late = via[rank] is not None

    def same_chip(a, b):
        return topo.host(a) == topo.host(b) and topo.chip(a) == topo.chip(b)

    def arr(q):
        return "arr%d" % topo.host(cores[q])

    own = [(r, near[r].index(rank)) for r in range(n) if rank in near[r]]
    passes_me = set(via[r] for r in range(n) if rank in far[r])
    own.sort(key=lambda e: (e[0] not in passes_me, same_chip(core, cores[e[0]]), e[0]))
    served = [r for r in range(n) if via[r] == rank]
    due = {}
    for q in box:
        due[arr(q)] = due.get(arr(q), 0) + E

    if own:
        g.sync.dma_start(T.xd[:], T.x[:]).then_inc(sem.copied, 16)
        g.scalar.wait_ge(sem.copied, 16)
    g.scalar.dma_start(T.xs[:], T.x[:]).then_inc(sem.loaded, 16)
    g.scalar.dma_start(T.us[:], T.u[:]).then_inc(sem.loaded, 16)
    if box:
        g.vector.memset(T.ones[0:k, :], 1.0).then_inc(sem.filled, 1)

    def ids(dests):
        out = []
        for d in dests:
            rid, pid = topo.addr(d, core)
            out.append(DstId(rid=rid, pnc=pid))
        return out

    sent = 0
    if own:
        dests = [cores[r] for r, s in own]
        g.wait_ge(sem.copied, 16)
        g.remote_dma_fused([RemoteDMATransfer(
            dst_ids=ids(dests), dma_engine_mask=_engines(topo, core, dests), remote_sem=sem[arr(rank)],
            srcs=[T.xd[t] for t in range(PIECES)], dsts=[T.land[s] for r, s in own], alu_op=1)], local_sem=sem.sent)
        sent += E
    if served:
        qs = far[served[0]]
        dests = [cores[r] for r in served]
        for name in sorted(set(arr(q) for q in qs)):
            g.wait_ge(sem[name], due[name])
        g.remote_dma_fused([RemoteDMATransfer(
            dst_ids=ids(dests), dma_engine_mask=_engines(topo, core, dests), remote_sem=sem.arrf,
            srcs=[T.land[box.index(q)] for q in qs], dsts=[T.farl[:] for r in served],
            alu_op=1 if len(qs) > 1 else 0)], local_sem=sem.sent)
        sent += E
    if sent:
        g.wait_ge(sem.sent, sent)

    if box:
        for name in sorted(due):
            g.sync.wait_ge(sem[name], due[name])
        g.sync.dma_start(T.lb[0:k, :], T.land[0:len(box)]).then_inc(sem.gathered, 16)
    if late:
        g.scalar.wait_ge(sem.arrf, E)
        g.scalar.dma_start(T.fb[0:ROWS, :], T.farl[:]).then_inc(sem.fetched, 16)

    g.tensor.wait_ge(sem.loaded, 32)
    mm = g.tensor.matmul(T.yp[:, 0:C], T.us[:], T.xs[:], True, not box)
    if box:
        g.tensor.wait_ge(sem.filled, 1)
        g.tensor.wait_ge(sem.gathered, 16)
        mm = g.tensor.matmul(T.yp[:, 0:C], T.ones[0:k, :], T.lb[0:k, :], False, not late)
    if late:
        g.tensor.wait_ge(sem.fetched, 16)
        mm = g.tensor.matmul(T.yp[:, 0:C], T.ones[0:ROWS, :], T.fb[0:ROWS, :], False, True)
    mm.then_inc(sem.summed, 1)

    g.vector.wait_ge(sem.summed, 1)
    g.vector.tensor_copy(T.ys[:], T.yp[:, 0:C]).then_inc(sem.rounded, 1)
    g.scalar.wait_ge(sem.rounded, 1)
    g.scalar.dma_start(T.y[:], T.ys[:]).then_inc(sem.stored, 16)
    g.scalar.wait_ge(sem.stored, 16)
